import numpy as np
import ml_dtypes


def mxq(x, axis, fmt="e4m3"):
    dtype, down = {"e4m3": (ml_dtypes.float8_e4m3fn, 7), "e5m2": (ml_dtypes.float8_e5m2, 14)}[fmt]
    v = np.moveaxis(np.asarray(x, np.float32).astype(ml_dtypes.bfloat16).astype(np.float64), axis, -1)
    blocks = v.reshape(v.shape[:-1] + (-1, 32))
    amax = np.abs(blocks).max(-1, keepdims=True)
    byte = np.maximum(np.where(amax > 0, np.frexp(amax)[1] - 1 + 127, 0) - down, 1)
    scale = np.exp2(byte - 127.0)
    codes = (blocks / scale).astype(np.float32).astype(dtype).astype(np.float64)
    return np.moveaxis((codes * scale).reshape(v.shape), -1, axis)


WIDE = False


def mx_kscale(k):
    if not WIDE:
        return np.ones(k)
    levels = np.array([10, -10, 5, -5, 0])
    if k % 512:
        return np.exp2(np.random.permutation(np.resize(levels, k // 32))).repeat(32)
    a = np.empty((k // 512, 16))
    for p in range(k // 512):
        a[p, :8] = np.random.permutation(np.resize(levels, 8))
        for g in range(8):
            far = levels[np.abs(levels - a[p, g]) >= 10]
            a[p, g + 8] = far[np.random.randint(len(far))]
    return np.exp2(a.ravel()).repeat(32)


def f64(x):
    return np.asarray(x).astype(np.float64)


def striped(idx):
    return np.tile(idx.reshape(-1, 16).T, (8, 1)).astype(np.uint16)


def unstriped(offs):
    return offs[:16].T.reshape(-1).astype(np.int64)


E2M1 = np.array([0.0, 0.5, 1.0, 1.5, 2.0, 3.0, 4.0, 6.0, -0.0, -0.5, -1.0, -1.5, -2.0, -3.0, -4.0, -6.0])


def pack_weight(w, fmt):
    k, n = w.shape
    w = f64(np.asarray(w, np.float32).astype(ml_dtypes.bfloat16)).reshape(k // 32, 32, n)
    amax = np.abs(w).max(1)
    if fmt == "e4m3":
        byte = np.frexp(amax)[1] - 1 + 127 - 7
    else:
        mant, ex = np.frexp(amax / 6.0)
        byte = np.where(mant > 0.5, ex, ex - 1) + 127
    byte = np.clip(np.where(amax > 0, byte, 1), 1, 254)
    scaled = (w * np.exp2(127.0 - byte)[:, None, :]).reshape(k, n).astype(np.float32)
    by_word = np.ascontiguousarray(scaled.reshape(k // 512, 128, 4, n).transpose(0, 1, 3, 2))
    if fmt == "e4m3":
        words = by_word.astype(ml_dtypes.float8_e4m3fn).view(np.uint8)
    else:
        c = by_word.astype(ml_dtypes.float4_e2m1fn).view(np.uint8) & 0xF
        words = (c[..., 0::2] | (c[..., 1::2] << 4)).reshape(k // 512, 128, 2 * n)
    return np.ascontiguousarray(words), np.ascontiguousarray(byte.astype(np.uint8).reshape(k // 512, 16, n))


def unpack_weight(words, scales, fmt):
    g, _, n = scales.shape
    words = np.ascontiguousarray(words).reshape(g, 128, n, -1)
    if fmt == "e4m3":
        vals = words.view(ml_dtypes.float8_e4m3fn).astype(np.float64)
    else:
        nib = np.empty((g, 128, n, 4), np.uint8)
        nib[..., 0::2] = words & 0xF
        nib[..., 1::2] = words >> 4
        vals = E2M1[nib]
    vals = vals * np.repeat(np.exp2(scales.astype(np.float64) - 127.0), 8, axis=1)[..., None]
    return vals.transpose(0, 1, 3, 2).reshape(g * 512, n)


def gelu(v):
    return 0.5 * v * (1.0 + np.tanh(np.sqrt(2.0 / np.pi) * (v + 0.044715 * v**3)))


K, T, S, S2 = 1024, 2048, 512, 1024


def setup_inputs():
    n = np.random.standard_normal
    s = mx_kscale(K)[:, None]
    d = {}
    d["tab_words"], d["tab_scales"] = pack_weight(n((K, T)) * s, "e4m3")
    d["offs"] = striped(np.random.permutation(T)[:S])
    d["offs2"] = striped(np.random.permutation(T)[:S2])
    base = 0.95 * n((K, K)) / K**0.5 / K**0.5 / s / s.T
    d["w4_words"], d["w4_scales"] = pack_weight(base, "e2m1")
    d["wfit"] = (0.7 * n((K, K)) / K**0.5 / K**0.5 / s / s.T).astype(np.float32)
    d["left"] = (0.8 * n(S2)).astype(np.float32)
    return d


def reference(tab_words, tab_scales, offs, offs2, w4_words, w4_scales, wfit, left):
    TW = unpack_weight(tab_words, tab_scales, "e4m3")
    v = TW[:, unstriped(offs)]
    v2 = TW[:, unstriped(offs2)]
    w4 = unpack_weight(w4_words, w4_scales, "e2m1")
    wq = mxq(f64(wfit), 0, "e4m3")
    h = np.abs(w4.T @ v + wq.T @ v)
    hq = mxq(h, 0, "e4m3")
    e = v2.T @ hq
    return np.tanh(e - f64(left)[:, None])

@@ -1,0 +1,250 @@
+from contextlib import ExitStack
+
+import concourse.mybir as mybir
+from concourse.masks import make_identity
+
+F32 = mybir.dt.float32
+BF16 = mybir.dt.bfloat16
+I32 = mybir.dt.int32
+U32 = mybir.dt.uint32
+U16 = mybir.dt.uint16
+U8 = mybir.dt.uint8
+FP8X4 = mybir.dt.float8_e4m3fn_x4
+FP4X4 = mybir.dt.float4_e2m1fn_x4
+ACT = mybir.ActivationFunctionType
+ALU = mybir.AluOpType
+
+P = 128
+K, T, S, S2 = 1024, 2048, 512, 1024
+KP = 512
+FLOPS = 2 * (2 * K * K * S + K * S2 * S)
+
+
+def tile_list_kerning_gap_suggester_kernel(
+    tc, tab_words, tab_scales, offs, offs2, w4_words, w4_scales, wfit, left, out
+):
+    nc = tc.nc
+    with ExitStack() as ctx:
+        keep = ctx.enter_context(tc.tile_pool(name="keep", bufs=1))
+        psum = ctx.enter_context(tc.psum_pool(name="psum", bufs=1))
+
+        def sb(name, shape, dtype, tag=None):
+            return keep.tile(shape, dtype, name=name, tag=tag or name, align_bytes=64)
+
+        def bank(n, name, shape):
+            return psum.tile(shape, F32, name=name, tag=f"bank{n}")
+
+        right_list = keep.tile([P, S // 16], U16, name="right_list")
+        left_list = keep.tile([P, S2 // 16], U16, name="left_list")
+        tab_s = sb("tab_s", [P, T], U8)
+        w4_s_raw = sb("w4_s_raw", [P, K], U8)
+        v_s = [sb(f"v_s{a}", [P, S], U8) for a in range(2)]
+        w4_s = [sb(f"w4_s{a}", [P, K], U8) for a in range(2)]
+        nc.vector.memset(tab_s[:].bitcast(I32), 0)
+        nc.gpsimd.memset(w4_s_raw[:].bitcast(I32), 0)
+        nc.vector.memset(v_s[1][:].bitcast(I32), 0)
+        nc.vector.memset(w4_s[1][:].bitcast(I32), 0)
+
+        w4_raw = sb("w4_raw", [P, 2 * K // 2], I32)
+        tab_w = {}
+        fit_raw = {}
+
+        def load_fit(a, b, tag=None):
+            raw = sb(f"fit_raw{a}{b}", [P, 4, KP], F32, tag)
+            fit_raw[a, b] = raw
+            rows = wfit[a * KP : (a + 1) * KP, b * KP : (b + 1) * KP]
+            nc.sync.dma_start(out=raw[:], in_=rows.rearrange("(p j) c -> p j c", j=4))
+
+        def load_tab(a, tag=None):
+            tab_w[a] = sb(f"tab_w{a}", [P, T], I32, tag)
+            nc.sync.dma_start(out=tab_w[a][:], in_=tab_words[a].rearrange("p t i -> p (t i)").bitcast(I32))
+
+        nc.sync.dma_start(right_list[:], offs)
+        nc.sync.dma_start(left_list[:], offs2)
+        nc.sync.dma_start(
+            out=w4_raw[:].rearrange("p (a c) -> p a c", a=2),
+            in_=w4_words.rearrange("a p c -> p a c").bitcast(I32),
+        )
+        for q in range(4):
+            nc.scalar.dma_start(
+                out=tab_s[32 * q : 32 * q + 8, :].bitcast(I32),
+                in_=tab_scales[:, 4 * q : 4 * q + 4, :].bitcast(I32),
+            )
+        load_fit(0, 0)
+        for q in range(4):
+            nc.gpsimd.dma_start(
+                out=w4_s_raw[32 * q : 32 * q + 8, :].bitcast(I32),
+                in_=w4_scales[:, 4 * q : 4 * q + 4, :].bitcast(I32),
+            )
+        load_tab(0)
+        left_rows = sb("left_rows", [P, P], F32)
+        ident = sb("ident", [P, P], F32)
+        nc.gpsimd.memset(left_rows[:], 0.0)
+        nc.gpsimd.dma_start(out=left_rows[0 : S2 // P, :], in_=left.rearrange("(m p) -> m p", p=P))
+        make_identity(nc, ident[:])
+
+        left_t = bank(7, "left_t", [P, P])
+        nc.tensor.transpose(left_t[:], left_rows[:], ident[:])
+        neg_left = sb("neg_left", [P, S2 // P], F32)
+        nc.scalar.mul(neg_left[:], left_t[:, 0 : S2 // P], -1.0)
+
+        def shift_plane(dst, src):
+            nc.gpsimd.dma_start(out=dst[0:100, :].bitcast(I32), in_=src[4:104, :].bitcast(I32))
+
+        w4_w = [sb(f"w4_w{a}", [P, K], U16) for a in range(2)]
+        for a in range(2):
+            nc.vector.tensor_copy(
+                out=w4_w[a][:].rearrange("p (b t q) -> p b q t", b=2, t=4),
+                in_=w4_raw[:, a * K // 2 : (a + 1) * K // 2].bitcast(U16).rearrange("p (b q t) -> p b q t", b=2, t=4),
+            )
+        load_fit(1, 0, "w4_raw")
+        nc.vector.tensor_copy(v_s[0][:], tab_s[:].indirect(right_list[:]))
+        shift_plane(v_s[1], v_s[0])
+        nc.vector.tensor_copy(
+            out=w4_s[0][:].rearrange("p (b t q) -> p b q t", b=2, t=4),
+            in_=w4_s_raw[:].rearrange("p (b q t) -> p b q t", b=2, t=4),
+        )
+        shift_plane(w4_s[1], w4_s[0])
+        load_tab(1, "w4_s_raw")
+
+        fit_bf, fit_w, fit_s = {}, {}, {}
+
+        def cast_fit(a, b, scalar_q):
+            bf = sb(f"fit_bf{a}{b}", [P, 4 * KP], BF16)
+            fit_bf[a, b] = bf
+            dst = bf[:].rearrange("p (t q j) -> p q j t", t=4, j=4)
+            src = fit_raw[a, b][:].rearrange("p j (q t) -> p q j t", t=4)
+            if scalar_q > 0:
+                nc.scalar.copy(out=dst[:, 0:scalar_q], in_=src[:, 0:scalar_q])
+            if scalar_q < P:
+                nc.vector.tensor_copy(out=dst[:, scalar_q:P], in_=src[:, scalar_q:P])
+
+        def quant_fit(a, b):
+            fit_w[a, b] = sb(f"fit_w{a}{b}", [P, KP], U32)
+            fit_s[a, b] = sb(f"fit_s{a}{b}", [P, KP], U8)
+            nc.vector.quantize_mx(out=fit_w[a, b][:].bitcast(FP8X4), scales=fit_s[a, b][:], in_=fit_bf[a, b][:])
+
+        v_w = [sb(f"v_w{a}", [P, S], U32) for a in range(2)]
+
+        def gather_v(a):
+            nc.vector.tensor_copy(v_w[a][:], tab_w[a][:].bitcast(U32).indirect(right_list[:]))
+
+        u_w, u_s = {}, {}
+
+        def gather_u_words(a, half):
+            u_w[a, half] = sb(f"u_w{a}{half}", [P, 512], U32)
+            nc.vector.tensor_copy(
+                u_w[a, half][:], tab_w[a][:].bitcast(U32).indirect(left_list[:, 32 * half : 32 * half + 32])
+            )
+
+        def gather_u_scales(half):
+            u_s[half] = sb(f"u_s{half}", [P, 512], U8)
+            nc.vector.tensor_copy(u_s[half][:], tab_s[:].indirect(left_list[:, 32 * half : 32 * half + 32]))
+
+        h_bank = {}
+
+        def stage1(kind, a, b, first=False, last=False):
+            for jc in range(4):
+                if first:
+                    h_bank[b, jc] = bank(4 * b + jc, f"h_bank{b}{jc}", [P, 4, P])
+                cols = slice(jc * P, (jc + 1) * P)
+                for t in range(4):
+                    if kind == "w4":
+                        r = slice(b * KP + t * P, b * KP + (t + 1) * P)
+                        lhsT, lhsT_scale = w4_w[a][:, r].bitcast(FP4X4), w4_s[a][:, r]
+                    else:
+                        r = slice(t * P, (t + 1) * P)
+                        lhsT, lhsT_scale = fit_w[a, b][:, r].bitcast(FP8X4), fit_s[a, b][:, r]
+                    nc.tensor.matmul_mx(
+                        out=h_bank[b, jc][:, t, :],
+                        lhsT=lhsT,
+                        lhsT_scale=lhsT_scale,
+                        rhs=v_w[a][:, cols].bitcast(FP8X4),
+                        rhs_scale=v_s[a][:, cols],
+                        start=first and t == 0,
+                        stop=last and t == 3,
+                    )
+
+        h_w = [sb(f"h_w{b}", [P, S], U32) for b in range(2)]
+        h_s = [sb(f"h_s{b}", [P, S], U8) for b in range(2)]
+        h_bf = {}
+
+        def abs_h(b, jc, on_vector=False):
+            bf = sb(f"h_bf{b}{jc}", [P, KP], BF16)
+            h_bf[b, jc] = bf
+            src = h_bank[b, jc][:].rearrange("p t j -> p j t")
+            if on_vector:
+                signed = sb(f"h_signed{b}{jc}", [P, KP], BF16)
+                nc.vector.tensor_copy(out=signed[:].rearrange("p (j t) -> p j t", t=4), in_=src)
+                nc.vector.scalar_tensor_tensor(bf[:], signed[:], -1.0, signed[:], ALU.mult, ALU.max)
+            else:
+                nc.scalar.activation(bf[:].rearrange("p (j t) -> p j t", t=4), src, ACT.Abs)
+
+        def quant_h(b, jc):
+            cols = slice(jc * P, (jc + 1) * P)
+            nc.vector.quantize_mx(out=h_w[b][:, cols].bitcast(FP8X4), scales=h_s[b][:, cols], in_=h_bf[b, jc][:])
+
+        e_bank = {}
+
+        def stage2(m, b):
+            if b == 0:
+                e_bank[m] = bank(m, f"e_bank{m}", [P, S])
+            cols = slice((m % 4) * P, (m % 4 + 1) * P)
+            nc.tensor.matmul_mx(
+                out=e_bank[m][:],
+                lhsT=u_w[b, m // 4][:, cols].bitcast(FP8X4),
+                lhsT_scale=u_s[m // 4][4 * b : P, cols],
+                rhs=h_w[b][:].bitcast(FP8X4),
+                rhs_scale=h_s[b][:],
+                start=b == 0,
+                stop=b == 1,
+            )
+
+        def finish(m):
+            res = sb(f"res{m}", [P, S], F32)
+            nc.scalar.activation(res[:], e_bank[m][:], ACT.Tanh, bias=neg_left[:, m : m + 1], scale=1.0)
+            nc.sync.dma_start(out=out[m * P : (m + 1) * P, :], in_=res[:])
+
+        cast_fit(0, 0, P)
+        load_fit(0, 1, "fit_raw00")
+        gather_u_scales(0)
+        gather_u_scales(1)
+        gather_v(0)
+        quant_fit(0, 0)
+        load_fit(1, 1, "fit_bf00")
+        stage1("w4", 0, 0, first=True)
+        stage1("fit", 0, 0)
+        stage1("w4", 0, 1, first=True)
+        gather_u_words(0, 0)
+        gather_u_words(0, 1)
+        cast_fit(1, 0, P)
+        gather_v(1)
+        quant_fit(1, 0)
+        stage1("w4", 1, 0)
+        stage1("fit", 1, 0, last=True)
+        stage1("w4", 1, 1)
+        for jc in range(4):
+            abs_h(0, jc)
+        cast_fit(0, 1, 0)
+        quant_fit(0, 1)
+        stage1("fit", 0, 1)
+        for jc in range(4):
+            quant_h(0, jc)
+        for m in range(4):
+            stage2(m, 0)
+        cast_fit(1, 1, 48)
+        quant_fit(1, 1)
+        stage1("fit", 1, 1, last=True)
+        for jc in range(4):
+            abs_h(1, jc, on_vector=jc == 3)
+        for jc in range(4):
+            quant_h(1, jc)
+        gather_u_words(1, 0)
+        for m in range(4):
+            stage2(m, 1)
+            finish(m)
+        gather_u_words(1, 1)
+        for m in range(4, 8):
+            stage2(m, 0)
+            stage2(m, 1)
+            finish(m)

@@ -37,27 +37,34 @@ def tile_list_kerning_gap_suggester_kernel(
         right_list = keep.tile([P, S // 16], U16, name="right_list")
         left_list = keep.tile([P, S2 // 16], U16, name="left_list")
         tab_s = sb("tab_s", [P, T], U8)
-        w4_s_raw = sb("w4_s_raw", [P, K], U8)
+        w4_s_raw = sb("w4_s_raw", [P, 2 * K], U8)
         v_s = [sb(f"v_s{a}", [P, S], U8) for a in range(2)]
         w4_s = [sb(f"w4_s{a}", [P, K], U8) for a in range(2)]
+        left_rows = sb("left_rows", [P, P], F32)
+        ident = sb("ident", [P, P], F32)
+        zero_rows = sb("zero_rows", [P, P], F32)
+        zero_words = sb("zero_words", [P, K // 2], I32)
         nc.vector.memset(tab_s[:].bitcast(I32), 0)
-        nc.gpsimd.memset(w4_s_raw[:].bitcast(I32), 0)
+        nc.vector.memset(zero_rows[:], 0.0)
+        nc.vector.memset(zero_words[:], 0)
+        nc.vector.tensor_copy(left_rows[:], zero_rows[:])
+        nc.vector.tensor_copy(w4_s_raw[:].bitcast(I32), zero_words[:])
         nc.vector.memset(v_s[1][:].bitcast(I32), 0)
-        nc.vector.memset(w4_s[1][:].bitcast(I32), 0)
+        make_identity(nc, ident[:])
 
-        w4_raw = sb("w4_raw", [P, 2 * K // 2], I32)
+        w4_raw = sb("w4_raw", [P, K], I32)
         tab_w = {}
         fit_raw = {}
 
-        def load_fit(a, b, tag=None):
-            raw = sb(f"fit_raw{a}{b}", [P, 4, KP], F32, tag)
+        def load_fit(a, b, tag):
+            raw = sb(f"fit_raw{a}{b}", [P, 4, KP], F32, tag)[:]
             fit_raw[a, b] = raw
             rows = wfit[a * KP : (a + 1) * KP, b * KP : (b + 1) * KP]
-            nc.sync.dma_start(out=raw[:], in_=rows.rearrange("(p j) c -> p j c", j=4))
+            nc.sync.dma_start(out=raw, in_=rows.rearrange("(p j) c -> p j c", j=4))
 
-        def load_tab(a, tag=None):
-            tab_w[a] = sb(f"tab_w{a}", [P, T], I32, tag)
-            nc.sync.dma_start(out=tab_w[a][:], in_=tab_words[a].rearrange("p t i -> p (t i)").bitcast(I32))
+        def load_tab(a):
+            tab_w[a] = sb(f"tab_w{a}", [P, T], I32, ("zero_words", "ident")[a])[:]
+            nc.sync.dma_start(out=tab_w[a], in_=tab_words[a].rearrange("p t i -> p (t i)").bitcast(I32))
 
         nc.sync.dma_start(right_list[:], offs)
         nc.sync.dma_start(left_list[:], offs2)
@@ -66,22 +73,18 @@ def tile_list_kerning_gap_suggester_kernel(
             in_=w4_words.rearrange("a p c -> p a c").bitcast(I32),
         )
         for q in range(4):
-            nc.scalar.dma_start(
+            nc.sync.dma_start(
                 out=tab_s[32 * q : 32 * q + 8, :].bitcast(I32),
                 in_=tab_scales[:, 4 * q : 4 * q + 4, :].bitcast(I32),
             )
-        load_fit(0, 0)
-        for q in range(4):
-            nc.gpsimd.dma_start(
-                out=w4_s_raw[32 * q : 32 * q + 8, :].bitcast(I32),
-                in_=w4_scales[:, 4 * q : 4 * q + 4, :].bitcast(I32),
-            )
+        load_fit(0, 0, "zero_rows")
         load_tab(0)
-        left_rows = sb("left_rows", [P, P], F32)
-        ident = sb("ident", [P, P], F32)
-        nc.gpsimd.memset(left_rows[:], 0.0)
+        for q in range(4):
+            nc.sync.dma_start(
+                out=w4_s_raw[32 * q : 32 * q + 4, :].bitcast(I32).rearrange("p (a c) -> p a c", a=2),
+                in_=w4_scales[:, 4 * q : 4 * q + 4, :].bitcast(I32).rearrange("a r c -> r a c"),
+            )
         nc.gpsimd.dma_start(out=left_rows[0 : S2 // P, :], in_=left.rearrange("(m p) -> m p", p=P))
-        make_identity(nc, ident[:])
 
         left_t = bank(7, "left_t", [P, P])
         nc.tensor.transpose(left_t[:], left_rows[:], ident[:])
@@ -89,8 +92,10 @@ def tile_list_kerning_gap_suggester_kernel(
         nc.scalar.mul(neg_left[:], left_t[:, 0 : S2 // P], -1.0)
 
         def shift_plane(dst, src):
-            nc.gpsimd.dma_start(out=dst[0:100, :].bitcast(I32), in_=src[4:104, :].bitcast(I32))
+            nc.sync.dma_start(out=dst[0:100, :].bitcast(I32), in_=src[4:104, :].bitcast(I32))
 
+        nc.vector.tensor_copy(v_s[0][:], tab_s[:].indirect(right_list[:]))
+        shift_plane(v_s[1], v_s[0])
         w4_w = [sb(f"w4_w{a}", [P, K], U16) for a in range(2)]
         for a in range(2):
             nc.vector.tensor_copy(
@@ -98,14 +103,14 @@ def tile_list_kerning_gap_suggester_kernel(
                 in_=w4_raw[:, a * K // 2 : (a + 1) * K // 2].bitcast(U16).rearrange("p (b q t) -> p b q t", b=2, t=4),
             )
         load_fit(1, 0, "w4_raw")
-        nc.vector.tensor_copy(v_s[0][:], tab_s[:].indirect(right_list[:]))
-        shift_plane(v_s[1], v_s[0])
-        nc.vector.tensor_copy(
-            out=w4_s[0][:].rearrange("p (b t q) -> p b q t", b=2, t=4),
-            in_=w4_s_raw[:].rearrange("p (b q t) -> p b q t", b=2, t=4),
-        )
-        shift_plane(w4_s[1], w4_s[0])
-        load_tab(1, "w4_s_raw")
+        load_tab(1)
+        load_fit(0, 1, "left_rows")
+
+        def deal_w4_scales(a):
+            nc.vector.tensor_copy(
+                out=w4_s[a][:].rearrange("p (b t q) -> p b q t", b=2, t=4),
+                in_=w4_s_raw[:, a * K : (a + 1) * K].rearrange("p (b q t) -> p b q t", b=2, t=4),
+            )
 
         fit_bf, fit_w, fit_s = {}, {}, {}
 
@@ -113,7 +118,7 @@ def tile_list_kerning_gap_suggester_kernel(
             bf = sb(f"fit_bf{a}{b}", [P, 4 * KP], BF16)
             fit_bf[a, b] = bf
             dst = bf[:].rearrange("p (t q j) -> p q j t", t=4, j=4)
-            src = fit_raw[a, b][:].rearrange("p j (q t) -> p q j t", t=4)
+            src = fit_raw[a, b].rearrange("p j (q t) -> p q j t", t=4)
             if scalar_q > 0:
                 nc.scalar.copy(out=dst[:, 0:scalar_q], in_=src[:, 0:scalar_q])
             if scalar_q < P:
@@ -127,14 +132,14 @@ def tile_list_kerning_gap_suggester_kernel(
         v_w = [sb(f"v_w{a}", [P, S], U32) for a in range(2)]
 
         def gather_v(a):
-            nc.vector.tensor_copy(v_w[a][:], tab_w[a][:].bitcast(U32).indirect(right_list[:]))
+            nc.vector.tensor_copy(v_w[a][:], tab_w[a].bitcast(U32).indirect(right_list[:]))
 
         u_w, u_s = {}, {}
 
-        def gather_u_words(a, half):
-            u_w[a, half] = sb(f"u_w{a}{half}", [P, 512], U32)
+        def gather_u_words(a, half, dst):
+            u_w[a, half] = dst
             nc.vector.tensor_copy(
-                u_w[a, half][:], tab_w[a][:].bitcast(U32).indirect(left_list[:, 32 * half : 32 * half + 32])
+                dst, tab_w[a].bitcast(U32).indirect(left_list[:, 32 * half : 32 * half + 32])
             )
 
         def gather_u_scales(half):
@@ -169,20 +174,19 @@ def tile_list_kerning_gap_suggester_kernel(
         h_s = [sb(f"h_s{b}", [P, S], U8) for b in range(2)]
         h_bf = {}
 
-        def abs_h(b, jc, on_vector=False):
-            bf = sb(f"h_bf{b}{jc}", [P, KP], BF16)
-            h_bf[b, jc] = bf
-            src = h_bank[b, jc][:].rearrange("p t j -> p j t")
-            if on_vector:
-                signed = sb(f"h_signed{b}{jc}", [P, KP], BF16)
-                nc.vector.tensor_copy(out=signed[:].rearrange("p (j t) -> p j t", t=4), in_=src)
-                nc.vector.scalar_tensor_tensor(bf[:], signed[:], -1.0, signed[:], ALU.mult, ALU.max)
-            else:
-                nc.scalar.activation(bf[:].rearrange("p (j t) -> p j t", t=4), src, ACT.Abs)
+        def abs_quant_h(b, jcs):
+            bf = sb(f"h_bf{b}{jcs[0]}", [P, KP * len(jcs)], BF16)
+            h_bf[b, jcs[0]] = bf
+            for n, jc in enumerate(jcs):
+                nc.scalar.activation(
+                    bf[:, n * KP : (n + 1) * KP].rearrange("p (j t) -> p j t", t=4),
+                    h_bank[b, jc][:].rearrange("p t j -> p j t"),
+                    ACT.Abs,
+                )
 
-        def quant_h(b, jc):
-            cols = slice(jc * P, (jc + 1) * P)
-            nc.vector.quantize_mx(out=h_w[b][:, cols].bitcast(FP8X4), scales=h_s[b][:, cols], in_=h_bf[b, jc][:])
+        def quant_h(b, jcs):
+            cols = slice(jcs[0] * P, (jcs[-1] + 1) * P)
+            nc.vector.quantize_mx(out=h_w[b][:, cols].bitcast(FP8X4), scales=h_s[b][:, cols], in_=h_bf[b, jcs[0]][:])
 
         e_bank = {}
 
@@ -206,44 +210,43 @@ def tile_list_kerning_gap_suggester_kernel(
             nc.sync.dma_start(out=out[m * P : (m + 1) * P, :], in_=res[:])
 
         cast_fit(0, 0, P)
-        load_fit(0, 1, "fit_raw00")
+        load_fit(1, 1, "zero_rows")
         gather_u_scales(0)
         gather_u_scales(1)
         gather_v(0)
         quant_fit(0, 0)
-        load_fit(1, 1, "fit_bf00")
-        stage1("w4", 0, 0, first=True)
-        stage1("fit", 0, 0)
+        stage1("fit", 0, 0, first=True)
+        gather_u_words(0, 0, sb("u_w00", [P, 512], U32)[:])
+        deal_w4_scales(0)
+        deal_w4_scales(1)
+        stage1("w4", 0, 0)
         stage1("w4", 0, 1, first=True)
-        gather_u_words(0, 0)
-        gather_u_words(0, 1)
         cast_fit(1, 0, P)
         gather_v(1)
         quant_fit(1, 0)
         stage1("w4", 1, 0)
         stage1("fit", 1, 0, last=True)
         stage1("w4", 1, 1)
-        for jc in range(4):
-            abs_h(0, jc)
+        abs_quant_h(0, [0, 1, 2, 3])
         cast_fit(0, 1, 0)
         quant_fit(0, 1)
         stage1("fit", 0, 1)
-        for jc in range(4):
-            quant_h(0, jc)
-        for m in range(4):
-            stage2(m, 0)
-        cast_fit(1, 1, 48)
+        cast_fit(1, 1, 32)
         quant_fit(1, 1)
         stage1("fit", 1, 1, last=True)
-        for jc in range(4):
-            abs_h(1, jc, on_vector=jc == 3)
-        for jc in range(4):
-            quant_h(1, jc)
-        gather_u_words(1, 0)
+        quant_h(0, [0, 1, 2, 3])
+        gather_u_words(1, 0, sb("u_w10", [P, 512], U32, "fit_bf11")[:])
+        for m in range(4):
+            stage2(m, 0)
+        for jcs in ([0, 1], [2], [3]):
+            abs_quant_h(1, jcs)
+            quant_h(1, jcs)
         for m in range(4):
             stage2(m, 1)
             finish(m)
-        gather_u_words(1, 1)
+        u_late = sb("u_late", [P, 1024], U32, "h_bf13")
+        gather_u_words(0, 1, u_late[:, 0:512])
+        gather_u_words(1, 1, u_late[:, 512:1024])
         for m in range(4, 8):
             stage2(m, 0)
             stage2(m, 1)

@@ -63,7 +63,7 @@ def tile_list_kerning_gap_suggester_kernel(
             nc.sync.dma_start(out=raw, in_=rows.rearrange("(p j) c -> p j c", j=4))
 
         def load_tab(a):
-            tab_w[a] = sb(f"tab_w{a}", [P, T], I32, ("zero_words", "ident")[a])[:]
+            tab_w[a] = sb(f"tab_w{a}", [P, T], I32, ("zero_rows", "w4_raw")[a])[:]
             nc.sync.dma_start(out=tab_w[a], in_=tab_words[a].rearrange("p t i -> p (t i)").bitcast(I32))
 
         nc.sync.dma_start(right_list[:], offs)
@@ -77,8 +77,8 @@ def tile_list_kerning_gap_suggester_kernel(
                 out=tab_s[32 * q : 32 * q + 8, :].bitcast(I32),
                 in_=tab_scales[:, 4 * q : 4 * q + 4, :].bitcast(I32),
             )
-        load_fit(0, 0, "zero_rows")
         load_tab(0)
+        load_fit(0, 0, "zero_words")
         for q in range(4):
             nc.sync.dma_start(
                 out=w4_s_raw[32 * q : 32 * q + 4, :].bitcast(I32).rearrange("p (a c) -> p a c", a=2),
@@ -92,24 +92,24 @@ def tile_list_kerning_gap_suggester_kernel(
         nc.scalar.mul(neg_left[:], left_t[:, 0 : S2 // P], -1.0)
 
         def shift_plane(dst, src):
-            nc.sync.dma_start(out=dst[0:100, :].bitcast(I32), in_=src[4:104, :].bitcast(I32))
+            nc.gpsimd.dma_start(out=dst[0:100, :].bitcast(I32), in_=src[4:104, :].bitcast(I32))
 
         nc.vector.tensor_copy(v_s[0][:], tab_s[:].indirect(right_list[:]))
         shift_plane(v_s[1], v_s[0])
         w4_w = [sb(f"w4_w{a}", [P, K], U16) for a in range(2)]
         for a in range(2):
             nc.vector.tensor_copy(
-                out=w4_w[a][:].rearrange("p (b t q) -> p b q t", b=2, t=4),
-                in_=w4_raw[:, a * K // 2 : (a + 1) * K // 2].bitcast(U16).rearrange("p (b q t) -> p b q t", b=2, t=4),
+                out=w4_w[a][:].rearrange("p (b t g q) -> p b g t q", b=2, t=4, q=8),
+                in_=w4_raw[:, a * K // 2 : (a + 1) * K // 2].bitcast(U16).rearrange("p (b g q t) -> p b g t q", b=2, t=4, q=8),
             )
-        load_fit(1, 0, "w4_raw")
         load_tab(1)
+        load_fit(1, 0, "ident")
         load_fit(0, 1, "left_rows")
 
         def deal_w4_scales(a):
             nc.vector.tensor_copy(
-                out=w4_s[a][:].rearrange("p (b t q) -> p b q t", b=2, t=4),
-                in_=w4_s_raw[:, a * K : (a + 1) * K].rearrange("p (b q t) -> p b q t", b=2, t=4),
+                out=w4_s[a][:].rearrange("p (b t g q) -> p b g t q", b=2, t=4, q=16),
+                in_=w4_s_raw[:, a * K : (a + 1) * K].rearrange("p (b g q t) -> p b g t q", b=2, t=4, q=16),
             )
 
         fit_bf, fit_w, fit_s = {}, {}, {}
@@ -209,23 +209,24 @@ def tile_list_kerning_gap_suggester_kernel(
             nc.scalar.activation(res[:], e_bank[m][:], ACT.Tanh, bias=neg_left[:, m : m + 1], scale=1.0)
             nc.sync.dma_start(out=out[m * P : (m + 1) * P, :], in_=res[:])
 
-        cast_fit(0, 0, P)
-        load_fit(1, 1, "zero_rows")
-        gather_u_scales(0)
-        gather_u_scales(1)
         gather_v(0)
-        quant_fit(0, 0)
-        stage1("fit", 0, 0, first=True)
-        gather_u_words(0, 0, sb("u_w00", [P, 512], U32)[:])
         deal_w4_scales(0)
         deal_w4_scales(1)
-        stage1("w4", 0, 0)
-        stage1("w4", 0, 1, first=True)
-        cast_fit(1, 0, P)
+        gather_u_scales(0)
+        gather_u_scales(1)
+        cast_fit(0, 0, P)
+        load_fit(1, 1, "zero_words")
+        quant_fit(0, 0)
         gather_v(1)
+        gather_u_words(0, 0, sb("u_w00", [P, 512], U32)[:])
+        gather_u_words(1, 0, sb("u_w10", [P, 512], U32)[:])
+        cast_fit(1, 0, 88)
         quant_fit(1, 0)
+        stage1("w4", 0, 0, first=True)
+        stage1("fit", 0, 0)
         stage1("w4", 1, 0)
         stage1("fit", 1, 0, last=True)
+        stage1("w4", 0, 1, first=True)
         stage1("w4", 1, 1)
         abs_quant_h(0, [0, 1, 2, 3])
         cast_fit(0, 1, 0)
@@ -235,7 +236,6 @@ def tile_list_kerning_gap_suggester_kernel(
         quant_fit(1, 1)
         stage1("fit", 1, 1, last=True)
         quant_h(0, [0, 1, 2, 3])
-        gather_u_words(1, 0, sb("u_w10", [P, 512], U32, "fit_bf11")[:])
         for m in range(4):
             stage2(m, 0)
         for jcs in ([0, 1], [2], [3]):

@@ -56,10 +56,10 @@ def tile_list_kerning_gap_suggester_kernel(
         tab_w = {}
         fit_raw = {}
 
-        def load_fit(a, b, tag):
-            raw = sb(f"fit_raw{a}{b}", [P, 4, KP], F32, tag)[:]
-            fit_raw[a, b] = raw
-            rows = wfit[a * KP : (a + 1) * KP, b * KP : (b + 1) * KP]
+        def load_fit(a, b, tag, q0=0, q1=P):
+            raw = sb(f"fit_raw{a}{b}_{q0}", [P, 4, 4 * (q1 - q0)], F32, tag)[:]
+            fit_raw[a, b, q0] = raw
+            rows = wfit[a * KP : (a + 1) * KP, b * KP + 4 * q0 : b * KP + 4 * q1]
             nc.sync.dma_start(out=raw, in_=rows.rearrange("(p j) c -> p j c", j=4))
 
         def load_tab(a):
@@ -114,15 +114,15 @@ def tile_list_kerning_gap_suggester_kernel(
 
         fit_bf, fit_w, fit_s = {}, {}, {}
 
-        def cast_fit(a, b, scalar_q):
-            bf = sb(f"fit_bf{a}{b}", [P, 4 * KP], BF16)
-            fit_bf[a, b] = bf
-            dst = bf[:].rearrange("p (t q j) -> p q j t", t=4, j=4)
-            src = fit_raw[a, b].rearrange("p j (q t) -> p q j t", t=4)
+        def cast_fit(a, b, scalar_q, q0=0, q1=P):
+            if q0 == 0:
+                fit_bf[a, b] = sb(f"fit_bf{a}{b}", [P, 4 * KP], BF16)
+            dst = fit_bf[a, b][:].rearrange("p (t q j) -> p q j t", t=4, j=4)[:, q0:q1]
+            src = fit_raw[a, b, q0].rearrange("p j (q t) -> p q j t", t=4)
             if scalar_q > 0:
                 nc.scalar.copy(out=dst[:, 0:scalar_q], in_=src[:, 0:scalar_q])
-            if scalar_q < P:
-                nc.vector.tensor_copy(out=dst[:, scalar_q:P], in_=src[:, scalar_q:P])
+            if scalar_q < q1 - q0:
+                nc.vector.tensor_copy(out=dst[:, scalar_q : q1 - q0], in_=src[:, scalar_q : q1 - q0])
 
         def quant_fit(a, b):
             fit_w[a, b] = sb(f"fit_w{a}{b}", [P, KP], U32)
@@ -212,14 +212,14 @@ def tile_list_kerning_gap_suggester_kernel(
         gather_v(0)
         deal_w4_scales(0)
         deal_w4_scales(1)
+        load_fit(1, 1, "w4_s_raw", 0, P // 2)
         gather_u_scales(0)
         gather_u_scales(1)
         cast_fit(0, 0, P)
-        load_fit(1, 1, "zero_words")
+        load_fit(1, 1, "zero_words", P // 2, P)
         quant_fit(0, 0)
         gather_v(1)
         gather_u_words(0, 0, sb("u_w00", [P, 512], U32)[:])
-        gather_u_words(1, 0, sb("u_w10", [P, 512], U32)[:])
         cast_fit(1, 0, 88)
         quant_fit(1, 0)
         stage1("w4", 0, 0, first=True)
@@ -228,14 +228,16 @@ def tile_list_kerning_gap_suggester_kernel(
         stage1("fit", 1, 0, last=True)
         stage1("w4", 0, 1, first=True)
         stage1("w4", 1, 1)
+        cast_fit(0, 1, 64)
         abs_quant_h(0, [0, 1, 2, 3])
-        cast_fit(0, 1, 0)
         quant_fit(0, 1)
         stage1("fit", 0, 1)
-        cast_fit(1, 1, 32)
+        cast_fit(1, 1, 0, 0, P // 2)
+        cast_fit(1, 1, 0, P // 2, P)
         quant_fit(1, 1)
         stage1("fit", 1, 1, last=True)
         quant_h(0, [0, 1, 2, 3])
+        gather_u_words(1, 0, sb("u_w10", [P, 512], U32, "fit_bf11")[:])
         for m in range(4):
             stage2(m, 0)
         for jcs in ([0, 1], [2], [3]):

from contextlib import ExitStack

import concourse.mybir as mybir
from concourse.masks import make_identity

F32 = mybir.dt.float32
BF16 = mybir.dt.bfloat16
I32 = mybir.dt.int32
U32 = mybir.dt.uint32
U16 = mybir.dt.uint16
U8 = mybir.dt.uint8
FP8X4 = mybir.dt.float8_e4m3fn_x4
FP4X4 = mybir.dt.float4_e2m1fn_x4
ACT = mybir.ActivationFunctionType
ALU = mybir.AluOpType

P = 128
K, T, S, S2 = 1024, 2048, 512, 1024
KP = 512
FLOPS = 2 * (2 * K * K * S + K * S2 * S)


def tile_list_kerning_gap_suggester_kernel(
    tc, tab_words, tab_scales, offs, offs2, w4_words, w4_scales, wfit, left, out
):
    nc = tc.nc
    with ExitStack() as ctx:
        keep = ctx.enter_context(tc.tile_pool(name="keep", bufs=1))
        psum = ctx.enter_context(tc.psum_pool(name="psum", bufs=1))

        def sb(name, shape, dtype, tag=None):
            return keep.tile(shape, dtype, name=name, tag=tag or name, align_bytes=64)

        def bank(n, name, shape):
            return psum.tile(shape, F32, name=name, tag=f"bank{n}")

        right_list = keep.tile([P, S // 16], U16, name="right_list")
        left_list = keep.tile([P, S2 // 16], U16, name="left_list")
        tab_s = sb("tab_s", [P, T], U8)
        w4_s_raw = sb("w4_s_raw", [P, 2 * K], U8)
        v_s = [sb(f"v_s{a}", [P, S], U8) for a in range(2)]
        w4_s = [sb(f"w4_s{a}", [P, K], U8) for a in range(2)]
        left_rows = sb("left_rows", [P, P], F32)
        ident = sb("ident", [P, P], F32)
        zero_rows = sb("zero_rows", [P, P], F32)
        zero_words = sb("zero_words", [P, K // 2], I32)
        nc.vector.memset(tab_s[:].bitcast(I32), 0)
        nc.vector.memset(zero_rows[:], 0.0)
        nc.vector.memset(zero_words[:], 0)
        nc.vector.tensor_copy(left_rows[:], zero_rows[:])
        nc.vector.tensor_copy(w4_s_raw[:].bitcast(I32), zero_words[:])
        nc.vector.memset(v_s[1][:].bitcast(I32), 0)
        make_identity(nc, ident[:])

        w4_raw = sb("w4_raw", [P, K], I32)
        tab_w = {}
        fit_raw = {}

        def load_fit(a, b, tag, q0=0, q1=P):
            raw = sb(f"fit_raw{a}{b}_{q0}", [P, 4, 4 * (q1 - q0)], F32, tag)[:]
            fit_raw[a, b, q0] = raw
            rows = wfit[a * KP : (a + 1) * KP, b * KP + 4 * q0 : b * KP + 4 * q1]
            nc.sync.dma_start(out=raw, in_=rows.rearrange("(p j) c -> p j c", j=4))

        def load_tab(a):
            tab_w[a] = sb(f"tab_w{a}", [P, T], I32, ("zero_rows", "w4_raw")[a])[:]
            nc.sync.dma_start(out=tab_w[a], in_=tab_words[a].rearrange("p t i -> p (t i)").bitcast(I32))

        nc.sync.dma_start(right_list[:], offs)
        nc.sync.dma_start(left_list[:], offs2)
        nc.sync.dma_start(
            out=w4_raw[:].rearrange("p (a c) -> p a c", a=2),
            in_=w4_words.rearrange("a p c -> p a c").bitcast(I32),
        )
        for q in range(4):
            nc.sync.dma_start(
                out=tab_s[32 * q : 32 * q + 8, :].bitcast(I32),
                in_=tab_scales[:, 4 * q : 4 * q + 4, :].bitcast(I32),
            )
        load_tab(0)
        load_fit(0, 0, "zero_words")
        for q in range(4):
            nc.sync.dma_start(
                out=w4_s_raw[32 * q : 32 * q + 4, :].bitcast(I32).rearrange("p (a c) -> p a c", a=2),
                in_=w4_scales[:, 4 * q : 4 * q + 4, :].bitcast(I32).rearrange("a r c -> r a c"),
            )
        nc.gpsimd.dma_start(out=left_rows[0 : S2 // P, :], in_=left.rearrange("(m p) -> m p", p=P))

        left_t = bank(7, "left_t", [P, P])
        nc.tensor.transpose(left_t[:], left_rows[:], ident[:])
        neg_left = sb("neg_left", [P, S2 // P], F32)
        nc.scalar.mul(neg_left[:], left_t[:, 0 : S2 // P], -1.0)

        def shift_plane(dst, src):
            nc.gpsimd.dma_start(out=dst[0:100, :].bitcast(I32), in_=src[4:104, :].bitcast(I32))

        nc.vector.tensor_copy(v_s[0][:], tab_s[:].indirect(right_list[:]))
        shift_plane(v_s[1], v_s[0])
        w4_w = [sb(f"w4_w{a}", [P, K], U16) for a in range(2)]
        for a in range(2):
            nc.vector.tensor_copy(
                out=w4_w[a][:].rearrange("p (b t g q) -> p b g t q", b=2, t=4, q=8),
                in_=w4_raw[:, a * K // 2 : (a + 1) * K // 2].bitcast(U16).rearrange("p (b g q t) -> p b g t q", b=2, t=4, q=8),
            )
        load_tab(1)
        load_fit(1, 0, "ident")
        load_fit(0, 1, "left_rows")

        def deal_w4_scales(a):
            nc.vector.tensor_copy(
                out=w4_s[a][:].rearrange("p (b t g q) -> p b g t q", b=2, t=4, q=16),
                in_=w4_s_raw[:, a * K : (a + 1) * K].rearrange("p (b g q t) -> p b g t q", b=2, t=4, q=16),
            )

        fit_bf, fit_w, fit_s = {}, {}, {}

        def cast_fit(a, b, scalar_q, q0=0, q1=P):
            if q0 == 0:
                fit_bf[a, b] = sb(f"fit_bf{a}{b}", [P, 4 * KP], BF16)
            dst = fit_bf[a, b][:].rearrange("p (t q j) -> p q j t", t=4, j=4)[:, q0:q1]
            src = fit_raw[a, b, q0].rearrange("p j (q t) -> p q j t", t=4)
            if scalar_q > 0:
                nc.scalar.copy(out=dst[:, 0:scalar_q], in_=src[:, 0:scalar_q])
            if scalar_q < q1 - q0:
                nc.vector.tensor_copy(out=dst[:, scalar_q : q1 - q0], in_=src[:, scalar_q : q1 - q0])

        def quant_fit(a, b):
            fit_w[a, b] = sb(f"fit_w{a}{b}", [P, KP], U32)
            fit_s[a, b] = sb(f"fit_s{a}{b}", [P, KP], U8)
            nc.vector.quantize_mx(out=fit_w[a, b][:].bitcast(FP8X4), scales=fit_s[a, b][:], in_=fit_bf[a, b][:])

        v_w = [sb(f"v_w{a}", [P, S], U32) for a in range(2)]

        def gather_v(a):
            nc.vector.tensor_copy(v_w[a][:], tab_w[a].bitcast(U32).indirect(right_list[:]))

        u_w, u_s = {}, {}

        def gather_u_words(a, half, dst):
            u_w[a, half] = dst
            nc.vector.tensor_copy(
                dst, tab_w[a].bitcast(U32).indirect(left_list[:, 32 * half : 32 * half + 32])
            )

        def gather_u_scales(half):
            u_s[half] = sb(f"u_s{half}", [P, 512], U8)
            nc.vector.tensor_copy(u_s[half][:], tab_s[:].indirect(left_list[:, 32 * half : 32 * half + 32]))

        h_bank = {}

        def stage1(kind, a, b, first=False, last=False):
            for jc in range(4):
                if first:
                    h_bank[b, jc] = bank(4 * b + jc, f"h_bank{b}{jc}", [P, 4, P])
                cols = slice(jc * P, (jc + 1) * P)
                for t in range(4):
                    if kind == "w4":
                        r = slice(b * KP + t * P, b * KP + (t + 1) * P)
                        lhsT, lhsT_scale = w4_w[a][:, r].bitcast(FP4X4), w4_s[a][:, r]
                    else:
                        r = slice(t * P, (t + 1) * P)
                        lhsT, lhsT_scale = fit_w[a, b][:, r].bitcast(FP8X4), fit_s[a, b][:, r]
                    nc.tensor.matmul_mx(
                        out=h_bank[b, jc][:, t, :],
                        lhsT=lhsT,
                        lhsT_scale=lhsT_scale,
                        rhs=v_w[a][:, cols].bitcast(FP8X4),
                        rhs_scale=v_s[a][:, cols],
                        start=first and t == 0,
                        stop=last and t == 3,
                    )

        h_w = [sb(f"h_w{b}", [P, S], U32) for b in range(2)]
        h_s = [sb(f"h_s{b}", [P, S], U8) for b in range(2)]
        h_bf = {}

        def abs_quant_h(b, jcs):
            bf = sb(f"h_bf{b}{jcs[0]}", [P, KP * len(jcs)], BF16)
            h_bf[b, jcs[0]] = bf
            for n, jc in enumerate(jcs):
                nc.scalar.activation(
                    bf[:, n * KP : (n + 1) * KP].rearrange("p (j t) -> p j t", t=4),
                    h_bank[b, jc][:].rearrange("p t j -> p j t"),
                    ACT.Abs,
                )

        def quant_h(b, jcs):
            cols = slice(jcs[0] * P, (jcs[-1] + 1) * P)
            nc.vector.quantize_mx(out=h_w[b][:, cols].bitcast(FP8X4), scales=h_s[b][:, cols], in_=h_bf[b, jcs[0]][:])

        e_bank = {}

        def stage2(m, b):
            if b == 0:
                e_bank[m] = bank(m, f"e_bank{m}", [P, S])
            cols = slice((m % 4) * P, (m % 4 + 1) * P)
            nc.tensor.matmul_mx(
                out=e_bank[m][:],
                lhsT=u_w[b, m // 4][:, cols].bitcast(FP8X4),
                lhsT_scale=u_s[m // 4][4 * b : P, cols],
                rhs=h_w[b][:].bitcast(FP8X4),
                rhs_scale=h_s[b][:],
                start=b == 0,
                stop=b == 1,
            )

        def finish(m):
            res = sb(f"res{m}", [P, S], F32)
            nc.scalar.activation(res[:], e_bank[m][:], ACT.Tanh, bias=neg_left[:, m : m + 1], scale=1.0)
            nc.sync.dma_start(out=out[m * P : (m + 1) * P, :], in_=res[:])

        gather_v(0)
        deal_w4_scales(0)
        deal_w4_scales(1)
        load_fit(1, 1, "w4_s_raw", 0, P // 2)
        gather_u_scales(0)
        gather_u_scales(1)
        cast_fit(0, 0, P)
        load_fit(1, 1, "zero_words", P // 2, P)
        quant_fit(0, 0)
        gather_v(1)
        gather_u_words(0, 0, sb("u_w00", [P, 512], U32)[:])
        cast_fit(1, 0, 88)
        quant_fit(1, 0)
        stage1("w4", 0, 0, first=True)
        stage1("fit", 0, 0)
        stage1("w4", 1, 0)
        stage1("fit", 1, 0, last=True)
        stage1("w4", 0, 1, first=True)
        stage1("w4", 1, 1)
        cast_fit(0, 1, 64)
        abs_quant_h(0, [0, 1, 2, 3])
        quant_fit(0, 1)
        stage1("fit", 0, 1)
        cast_fit(1, 1, 0, 0, P // 2)
        cast_fit(1, 1, 0, P // 2, P)
        quant_fit(1, 1)
        stage1("fit", 1, 1, last=True)
        quant_h(0, [0, 1, 2, 3])
        gather_u_words(1, 0, sb("u_w10", [P, 512], U32, "fit_bf11")[:])
        for m in range(4):
            stage2(m, 0)
        for jcs in ([0, 1], [2], [3]):
            abs_quant_h(1, jcs)
            quant_h(1, jcs)
        for m in range(4):
            stage2(m, 1)
            finish(m)
        u_late = sb("u_late", [P, 1024], U32, "h_bf13")
        gather_u_words(0, 1, u_late[:, 0:512])
        gather_u_words(1, 1, u_late[:, 512:1024])
        for m in range(4, 8):
            stage2(m, 0)
            stage2(m, 1)
            finish(m)
